import numpy as np
import ml_dtypes


def mxq(x, axis, fmt="e4m3"):
    dtype, down = {"e4m3": (ml_dtypes.float8_e4m3fn, 7), "e5m2": (ml_dtypes.float8_e5m2, 14)}[fmt]
    v = np.moveaxis(np.asarray(x, np.float32).astype(ml_dtypes.bfloat16).astype(np.float64), axis, -1)
    blocks = v.reshape(v.shape[:-1] + (-1, 32))
    amax = np.abs(blocks).max(-1, keepdims=True)
    byte = np.maximum(np.where(amax > 0, np.frexp(amax)[1] - 1 + 127, 0) - down, 1)
    scale = np.exp2(byte - 127.0)
    codes = (blocks / scale).astype(np.float32).astype(dtype).astype(np.float64)
    return np.moveaxis((codes * scale).reshape(v.shape), -1, axis)


WIDE = False


def mx_kscale(k):
    if not WIDE:
        return np.ones(k)
    levels = np.array([24, -24, 12, -12, 0])
    if k % 512:
        return np.exp2(np.random.permutation(np.resize(levels, k // 32))).repeat(32)
    a = np.empty((k // 512, 16))
    for p in range(k // 512):
        a[p, :8] = np.random.permutation(np.resize(levels, 8))
        for g in range(8):
            far = levels[np.abs(levels - a[p, g]) >= 10]
            a[p, g + 8] = far[np.random.randint(len(far))]
    return np.exp2(a.ravel()).repeat(32)


def f64(x):
    return np.asarray(x).astype(np.float64)


def striped(idx):
    return np.tile(idx.reshape(-1, 16).T, (8, 1)).astype(np.uint16)


def unstriped(offs):
    return offs[:16].T.reshape(-1).astype(np.int64)


E2M1 = np.array([0.0, 0.5, 1.0, 1.5, 2.0, 3.0, 4.0, 6.0, -0.0, -0.5, -1.0, -1.5, -2.0, -3.0, -4.0, -6.0])


def pack_weight(w, fmt):
    k, n = w.shape
    w = f64(np.asarray(w, np.float32).astype(ml_dtypes.bfloat16)).reshape(k // 32, 32, n)
    amax = np.abs(w).max(1)
    if fmt == "e4m3":
        byte = np.frexp(amax)[1] - 1 + 127 - 7
    else:
        mant, ex = np.frexp(amax / 6.0)
        byte = np.where(mant > 0.5, ex, ex - 1) + 127
    byte = np.clip(np.where(amax > 0, byte, 1), 1, 254)
    scaled = (w * np.exp2(127.0 - byte)[:, None, :]).reshape(k, n).astype(np.float32)
    by_word = np.ascontiguousarray(scaled.reshape(k // 512, 128, 4, n).transpose(0, 1, 3, 2))
    if fmt == "e4m3":
        words = by_word.astype(ml_dtypes.float8_e4m3fn).view(np.uint8)
    else:
        c = by_word.astype(ml_dtypes.float4_e2m1fn).view(np.uint8) & 0xF
        words = (c[..., 0::2] | (c[..., 1::2] << 4)).reshape(k // 512, 128, 2 * n)
    return np.ascontiguousarray(words), np.ascontiguousarray(byte.astype(np.uint8).reshape(k // 512, 16, n))


def unpack_weight(words, scales, fmt):
    g, _, n = scales.shape
    words = np.ascontiguousarray(words).reshape(g, 128, n, -1)
    if fmt == "e4m3":
        vals = words.view(ml_dtypes.float8_e4m3fn).astype(np.float64)
    else:
        nib = np.empty((g, 128, n, 4), np.uint8)
        nib[..., 0::2] = words & 0xF
        nib[..., 1::2] = words >> 4
        vals = E2M1[nib]
    vals = vals * np.repeat(np.exp2(scales.astype(np.float64) - 127.0), 8, axis=1)[..., None]
    return vals.transpose(0, 1, 3, 2).reshape(g * 512, n)


def silu(f):
    return f / (1.0 + np.exp(-np.maximum(f, -700.0)))


K, L, N, T, J = 512, 512, 512, 4096, 512


def setup_inputs():
    n = np.random.standard_normal
    s = mx_kscale(K)[:, None]
    s2 = mx_kscale(L)[:, None]
    p_tab = pack_weight(n((K, T)) * s, "e4m3")
    p_w = pack_weight(n((K, N)) / np.sqrt(K) / s, "e2m1")
    p_wx = pack_weight(n((L, N)) / np.sqrt(L) / s2, "e4m3")
    return {
        "tab_words": p_tab[0],
        "tab_scales": p_tab[1],
        "w_words": p_w[0],
        "w_scales": p_w[1],
        "x": (n((L, J)) * s2).astype(np.float32),
        "wx_words": p_wx[0],
        "wx_scales": p_wx[1],
        "iw0": (np.random.uniform(0.1, 0.6, J)).astype(np.float32),
        "iw1": (np.random.uniform(0.1, 0.6, J)).astype(np.float32),
        "iw2": (np.random.uniform(0.1, 0.6, J)).astype(np.float32),
        "iw3": (np.random.uniform(0.1, 0.6, J)).astype(np.float32),
        "b": (0.3 * n(N)).astype(np.float32),
        "offs": striped(np.concatenate([np.random.permutation(T)[:J] for _ in range(4)])),
    }


def reference(tab_words, tab_scales, w_words, w_scales, x, wx_words, wx_scales, iw0, iw1, iw2, iw3, b, offs):
    idx = unstriped(offs).reshape(4, J)
    tab_ = unpack_weight(tab_words, tab_scales, "e4m3")[:, idx]
    w_ = unpack_weight(w_words, w_scales, "e2m1")
    a0 = w_.T @ tab_[:, 0]
    a1 = w_.T @ tab_[:, 1]
    a2 = w_.T @ tab_[:, 2]
    a3 = w_.T @ tab_[:, 3]
    x_ = mxq(f64(x), 0, "e4m3")
    wx_ = unpack_weight(wx_words, wx_scales, "e4m3")
    ax = wx_.T @ x_
    return silu(a0 * f64(iw0)[None, :] + a1 * f64(iw1)[None, :] + a2 * f64(iw2)[None, :] + a3 * f64(iw3)[None, :] + ax + f64(b)[:, None])

@@ -1,0 +1,164 @@
+from contextlib import ExitStack
+
+import concourse.mybir as mybir
+from concourse.masks import make_identity
+
+K, L, N, T, J = 512, 512, 512, 4096, 512
+G = 4
+P = 128
+FLOPS = 2 * K * N * J * G + 2 * L * N * J
+
+F32 = mybir.dt.float32
+BF16 = mybir.dt.bfloat16
+I32 = mybir.dt.int32
+U32 = mybir.dt.uint32
+U16 = mybir.dt.uint16
+U8 = mybir.dt.uint8
+FP8X4 = mybir.dt.float8_e4m3fn_x4
+FP4X4 = mybir.dt.float4_e2m1fn_x4
+ACT = mybir.ActivationFunctionType
+ALU = mybir.AluOpType
+
+JB = J // P
+NB = N // P
+HALF = J // 2
+MX_BANKS = 4
+
+
+def load_scale_rows(queues, plane, rows):
+    for r, queue in enumerate(queues):
+        queue.dma_start(out=plane[r:P:32, :].bitcast(I32), in_=rows[r:16:4, :].bitcast(I32))
+
+
+def tile_list_interp_silu_kernel(
+    tc, tab_words, tab_scales, w_words, w_scales, x, wx_words, wx_scales, iw0, iw1, iw2, iw3, b, offs, out
+):
+    nc = tc.nc
+    with ExitStack() as ctx:
+        keep = ctx.enter_context(tc.tile_pool(name="keep", bufs=1))
+        psum = ctx.enter_context(tc.psum_pool(name="psum", bufs=1))
+
+        offsets = keep.tile([P, G * J // 16], U16, name="offsets")
+        tab_w = keep.tile([P, T], U32, name="tab_w", align_bytes=64)
+        tab_s = keep.tile([P, T], U8, name="tab_s", align_bytes=64)
+        w_w = keep.tile([P, 2 * N], U8, name="w_w", align_bytes=64)
+        w_s = keep.tile([P, N], U8, name="w_s", align_bytes=64)
+        wx_w = keep.tile([P, N], U32, name="wx_w", align_bytes=64)
+        wx_s = keep.tile([P, N], U8, name="wx_s", align_bytes=64)
+        x_raw = [keep.tile([P, 4, HALF], F32, name="x_raw%d" % h) for h in range(2)]
+        x_w = [keep.tile([P, HALF], U32, name="x_w%d" % h, align_bytes=64) for h in range(2)]
+        x_s = [keep.tile([P, HALF], U8, name="x_s%d" % h, align_bytes=64) for h in range(2)]
+        got_w = [keep.tile([P, J], U32, name="got_w%d" % g, align_bytes=64) for g in range(G)]
+        rows = keep.tile([P, P], F32, name="rows")
+        cols = keep.tile([P, (G + 1) * 4], F32, name="cols")
+        ident = keep.tile([P, P], F32, name="ident")
+        warm = keep.tile([P, 16], F32, name="warm")
+        mx_bank = [psum.tile([P, N], F32, name="mx_bank%d" % i) for i in range(MX_BANKS)]
+        sum_bank = [psum.tile([P, N], F32, name="sum_bank%d" % i) for i in range(JB)]
+
+        tab_s_words = tab_s[:].bitcast(I32)
+        nc.vector.memset(tab_s_words[:, 0:768], 0)
+        nc.gpsimd.memset(tab_s_words[:, 768:1024], 0)
+        nc.gpsimd.memset(warm[:, 0:1], 0.0)
+        nc.gpsimd.memset(wx_s[:].bitcast(I32), 0)
+        nc.gpsimd.memset(rows[:], 0.0)
+        nc.gpsimd.memset(w_s[:].bitcast(I32), 0)
+        make_identity(nc, ident[:])
+
+        x_rows = x.rearrange("(p t) j -> p t j", t=4)
+        nc.sync.dma_start(offsets[:], offs)
+        nc.sync.dma_start(out=wx_w[:].bitcast(I32), in_=wx_words[0].rearrange("p n i -> p (n i)").bitcast(I32))
+        nc.sync.dma_start(out=w_w[:].bitcast(I32), in_=w_words[0].bitcast(I32))
+        load_scale_rows((nc.sync,) * 4, tab_s, tab_scales[0])
+        for h in range(2):
+            nc.sync.dma_start(out=x_raw[h][:], in_=x_rows[:, :, h * HALF : (h + 1) * HALF])
+        load_scale_rows((nc.sync,) * 4, wx_s, wx_scales[0])
+        nc.sync.dma_start(out=tab_w[:].bitcast(I32), in_=tab_words[0].rearrange("p t i -> p (t i)").bitcast(I32))
+        load_scale_rows((nc.sync,) * 4, w_s, w_scales[0])
+        for i, vec in enumerate((iw0, iw1, iw2, iw3, b)):
+            queue = nc.gpsimd if i < 2 else nc.sync
+            queue.dma_start(out=rows[4 * i : 4 * i + 4, :], in_=vec.rearrange("(c p) -> c p", p=P))
+
+        nc.scalar.activation(out=warm[:, 8:9], in_=warm[:, 0:1], func=ACT.Silu)
+
+        got_s = []
+
+        def gather_scales(tag):
+            g = len(got_s)
+            got = keep.tile([P, J], U8, name="got_s%d" % g, tag=tag, align_bytes=64)
+            got_s.append(got)
+            nc.vector.tensor_copy(got[:], tab_s[:].indirect(offsets[:, 32 * g : 32 * (g + 1)]))
+
+        gather_scales("got_s0")
+        gather_scales("got_s1")
+        for h in range(2):
+            x_bf = keep.tile([P, HALF, 4], BF16, name="x_bf%d" % h, tag="stage%d" % h, align_bytes=64)
+            nc.scalar.copy(
+                out=x_bf[:].rearrange("p (c i) t -> p c t i", i=4),
+                in_=x_raw[h][:].rearrange("p t (c i) -> p c t i", i=4),
+            )
+            nc.vector.quantize_mx(
+                out=x_w[h][:].bitcast(FP8X4), scales=x_s[h][:], in_=x_bf[:].rearrange("p c t -> p (c t)")
+            )
+            gather_scales("stage%d" % h)
+        for g in range(G):
+            nc.vector.tensor_copy(got_w[g][:], tab_w[:].indirect(offsets[:, 32 * g : 32 * (g + 1)]))
+
+
+        steps = [(G, jb, "s") for jb in range(JB)]
+        steps = steps + [(0, jb, "s") for jb in range(JB)]
+        steps = steps + [(1, 0, "s"), (1, 1, "s"), (2, 0, "v"), (1, 2, "s"), (2, 1, "v"), (1, 3, "s"), (3, 0, "v"),
+                         (2, 3, "s"), (2, 2, "v"), (3, 1, "v"), (3, 3, "v"), (3, 2, "v")]
+        merged = set((g - 1, jb) for g, jb, e in steps if e == "v")
+        part = {}
+
+        def product(n):
+            g, jb, e = steps[n]
+            bank = mx_bank[n % MX_BANKS]
+            if g == G:
+                h, c = divmod(jb * P, HALF)
+                nc.tensor.matmul_mx(bank[:], lhsT=x_w[h][:, c : c + P].bitcast(FP8X4), lhsT_scale=x_s[h][:, c : c + P],
+                                    rhs=wx_w[:].bitcast(FP8X4), rhs_scale=wx_s[:], start=True, stop=True)
+            else:
+                js = slice(jb * P, (jb + 1) * P)
+                nc.tensor.matmul_mx(bank[:], lhsT=got_w[g][:, js].bitcast(FP8X4), lhsT_scale=got_s[g][:, js],
+                                    rhs=w_w[:].bitcast(FP4X4), rhs_scale=w_s[:], start=True, stop=True)
+
+        def weigh(n):
+            g, jb, e = steps[n]
+            bank = mx_bank[n % MX_BANKS]
+            dst = keep.tile([P, N], F32, name="part%d_%d" % (g, jb))
+            part[g, jb] = dst
+            if g == G:
+                nc.scalar.copy(out=dst[:], in_=bank[:])
+            elif e == "s":
+                nc.scalar.activation(out=dst[:], in_=bank[:], func=ACT.Copy, scale=cols[:, 4 * g + jb : 4 * g + jb + 1])
+            else:
+                nc.vector.scalar_tensor_tensor(out=dst[:], in0=bank[:], scalar=cols[:, 4 * g + jb : 4 * g + jb + 1],
+                                               in1=part[g - 1, jb][:], op0=ALU.mult, op1=ALU.add)
+
+        def turn(n):
+            g, jb, e = steps[n]
+            if (g, jb) in merged:
+                return
+            for nb in range(NB):
+                ns = slice(nb * P, (nb + 1) * P)
+                nc.tensor.matmul(sum_bank[jb][:, ns], lhsT=part[g, jb][:, ns], rhs=ident[:], is_transpose=True,
+                                 start=(g == G and nb == 0), stop=(g == G - 1 and nb == NB - 1))
+            if g == G - 1:
+                res = keep.tile([P, NB, P], F32, name="res%d" % jb)
+                for nb in range(NB):
+                    nc.scalar.activation(out=res[:, nb, :], in_=sum_bank[jb][:, nb * P : (nb + 1) * P], func=ACT.Silu,
+                                         bias=cols[:, 4 * G + nb : 4 * G + nb + 1])
+                nc.sync.dma_start(out=out.rearrange("(c p) j -> p c j", p=P)[:, :, jb * P : (jb + 1) * P], in_=res[:])
+
+        for n in range(MX_BANKS):
+            product(n)
+        for n in range(len(steps)):
+            weigh(n)
+            if n == JB - 1:
+                nc.tensor.transpose(mx_bank[n][:, 0:P], rows[:], ident[:])
+                nc.scalar.copy(out=cols[:], in_=mx_bank[n][:, 0 : (G + 1) * 4])
+            if n + MX_BANKS < len(steps):
+                product(n + MX_BANKS)
+            turn(n)

@@ -23,6 +23,8 @@ JB = J // P
 NB = N // P
 HALF = J // 2
 MX_BANKS = 4
+SKIP = G
+EARLY = HALF // P
 
 
 def load_scale_rows(queues, plane, rows):
@@ -46,7 +48,8 @@ def tile_list_interp_silu_kernel(
         wx_w = keep.tile([P, N], U32, name="wx_w", align_bytes=64)
         wx_s = keep.tile([P, N], U8, name="wx_s", align_bytes=64)
         x_raw = [keep.tile([P, 4, HALF], F32, name="x_raw%d" % h) for h in range(2)]
-        x_w = [keep.tile([P, HALF], U32, name="x_w%d" % h, align_bytes=64) for h in range(2)]
+        x_bf = [keep.tile([P, HALF, 4], BF16, name="x_bf%d" % h, align_bytes=64) for h in range(2)]
+        got_s = [keep.tile([P, J], U8, name="got_s%d" % g, align_bytes=64) for g in range(G)]
         x_s = [keep.tile([P, HALF], U8, name="x_s%d" % h, align_bytes=64) for h in range(2)]
         got_w = [keep.tile([P, J], U32, name="got_w%d" % g, align_bytes=64) for g in range(G)]
         rows = keep.tile([P, P], F32, name="rows")
@@ -67,55 +70,41 @@ def tile_list_interp_silu_kernel(
 
         x_rows = x.rearrange("(p t) j -> p t j", t=4)
         nc.sync.dma_start(offsets[:], offs)
-        nc.sync.dma_start(out=wx_w[:].bitcast(I32), in_=wx_words[0].rearrange("p n i -> p (n i)").bitcast(I32))
-        nc.sync.dma_start(out=w_w[:].bitcast(I32), in_=w_words[0].bitcast(I32))
+        nc.sync.dma_start(out=x_raw[0][:], in_=x_rows[:, :, 0:HALF])
         load_scale_rows((nc.sync,) * 4, tab_s, tab_scales[0])
-        for h in range(2):
-            nc.sync.dma_start(out=x_raw[h][:], in_=x_rows[:, :, h * HALF : (h + 1) * HALF])
+        nc.sync.dma_start(out=wx_w[:].bitcast(I32), in_=wx_words[0].rearrange("p n i -> p (n i)").bitcast(I32))
+        nc.sync.dma_start(out=x_raw[1][:], in_=x_rows[:, :, HALF:J])
         load_scale_rows((nc.sync,) * 4, wx_s, wx_scales[0])
         nc.sync.dma_start(out=tab_w[:].bitcast(I32), in_=tab_words[0].rearrange("p t i -> p (t i)").bitcast(I32))
-        load_scale_rows((nc.sync,) * 4, w_s, w_scales[0])
         for i, vec in enumerate((iw0, iw1, iw2, iw3, b)):
-            queue = nc.gpsimd if i < 2 else nc.sync
+            queue = nc.sync if i in (2, 3) else nc.gpsimd
             queue.dma_start(out=rows[4 * i : 4 * i + 4, :], in_=vec.rearrange("(c p) -> c p", p=P))
+        nc.sync.dma_start(out=w_w[:].bitcast(I32), in_=w_words[0].bitcast(I32))
+        load_scale_rows((nc.sync,) * 4, w_s, w_scales[0])
 
         nc.scalar.activation(out=warm[:, 8:9], in_=warm[:, 0:1], func=ACT.Silu)
 
-        got_s = []
-
-        def gather_scales(tag):
-            g = len(got_s)
-            got = keep.tile([P, J], U8, name="got_s%d" % g, tag=tag, align_bytes=64)
-            got_s.append(got)
-            nc.vector.tensor_copy(got[:], tab_s[:].indirect(offsets[:, 32 * g : 32 * (g + 1)]))
-
-        gather_scales("got_s0")
-        gather_scales("got_s1")
-        for h in range(2):
-            x_bf = keep.tile([P, HALF, 4], BF16, name="x_bf%d" % h, tag="stage%d" % h, align_bytes=64)
-            nc.scalar.copy(
-                out=x_bf[:].rearrange("p (c i) t -> p c t i", i=4),
-                in_=x_raw[h][:].rearrange("p t (c i) -> p c t i", i=4),
-            )
-            nc.vector.quantize_mx(
-                out=x_w[h][:].bitcast(FP8X4), scales=x_s[h][:], in_=x_bf[:].rearrange("p c t -> p (c t)")
-            )
-            gather_scales("stage%d" % h)
-        for g in range(G):
-            nc.vector.tensor_copy(got_w[g][:], tab_w[:].indirect(offsets[:, 32 * g : 32 * (g + 1)]))
-
-
-        steps = [(G, jb, "s") for jb in range(JB)]
-        steps = steps + [(0, jb, "s") for jb in range(JB)]
-        steps = steps + [(1, 0, "s"), (1, 1, "s"), (2, 0, "v"), (1, 2, "s"), (2, 1, "v"), (1, 3, "s"), (3, 0, "v"),
-                         (2, 3, "s"), (2, 2, "v"), (3, 1, "v"), (3, 3, "v"), (3, 2, "v")]
-        merged = set((g - 1, jb) for g, jb, e in steps if e == "v")
+        x_w = []
         part = {}
 
-        def product(n):
-            g, jb, e = steps[n]
-            bank = mx_bank[n % MX_BANKS]
-            if g == G:
+        def interleave_half(h, copy):
+            copy(
+                out=x_bf[h][:].rearrange("p (c i) t -> p c t i", i=4),
+                in_=x_raw[h][:].rearrange("p t (c i) -> p c t i", i=4),
+            )
+
+        def quantise_half(h, tag):
+            words = keep.tile([P, HALF], U32, name="x_w%d" % h, tag=tag, align_bytes=64)
+            x_w.append(words)
+            nc.vector.quantize_mx(
+                out=words[:].bitcast(FP8X4), scales=x_s[h][:], in_=x_bf[h][:].rearrange("p c t -> p (c t)")
+            )
+
+        def weight(g, jb):
+            return cols[:, 4 * g + jb : 4 * g + jb + 1]
+
+        def product(g, jb, bank):
+            if g == SKIP:
                 h, c = divmod(jb * P, HALF)
                 nc.tensor.matmul_mx(bank[:], lhsT=x_w[h][:, c : c + P].bitcast(FP8X4), lhsT_scale=x_s[h][:, c : c + P],
                                     rhs=wx_w[:].bitcast(FP8X4), rhs_scale=wx_s[:], start=True, stop=True)
@@ -124,41 +113,72 @@ def tile_list_interp_silu_kernel(
                 nc.tensor.matmul_mx(bank[:], lhsT=got_w[g][:, js].bitcast(FP8X4), lhsT_scale=got_s[g][:, js],
                                     rhs=w_w[:].bitcast(FP4X4), rhs_scale=w_s[:], start=True, stop=True)
 
-        def weigh(n):
-            g, jb, e = steps[n]
-            bank = mx_bank[n % MX_BANKS]
-            dst = keep.tile([P, N], F32, name="part%d_%d" % (g, jb))
-            part[g, jb] = dst
-            if g == G:
-                nc.scalar.copy(out=dst[:], in_=bank[:])
-            elif e == "s":
-                nc.scalar.activation(out=dst[:], in_=bank[:], func=ACT.Copy, scale=cols[:, 4 * g + jb : 4 * g + jb + 1])
-            else:
-                nc.vector.scalar_tensor_tensor(out=dst[:], in0=bank[:], scalar=cols[:, 4 * g + jb : 4 * g + jb + 1],
-                                               in1=part[g - 1, jb][:], op0=ALU.mult, op1=ALU.add)
+        def new_part(key, jb):
+            dst = keep.tile([P, N], F32, name="part%s_%d" % (key, jb), tag="part%s_%d" % (key, jb), align_bytes=64)
+            part[key, jb] = dst
+            return dst
 
-        def turn(n):
-            g, jb, e = steps[n]
-            if (g, jb) in merged:
-                return
+        def weigh(g, jb, bank):
+            dst = new_part(g, jb)
+            if g == SKIP:
+                nc.scalar.copy(out=dst[:], in_=bank[:])
+            elif g < 2:
+                nc.scalar.activation(out=dst[:], in_=bank[:], func=ACT.Copy, scale=weight(g, jb))
+            else:
+                onto = 0 if g == 2 and jb >= EARLY else g - 1
+                nc.vector.scalar_tensor_tensor(out=dst[:], in0=bank[:], scalar=weight(g, jb),
+                                               in1=part[onto, jb][:], op0=ALU.mult, op1=ALU.add)
+
+        def turn(key, jb, start, stop):
             for nb in range(NB):
                 ns = slice(nb * P, (nb + 1) * P)
-                nc.tensor.matmul(sum_bank[jb][:, ns], lhsT=part[g, jb][:, ns], rhs=ident[:], is_transpose=True,
-                                 start=(g == G and nb == 0), stop=(g == G - 1 and nb == NB - 1))
-            if g == G - 1:
-                res = keep.tile([P, NB, P], F32, name="res%d" % jb)
-                for nb in range(NB):
-                    nc.scalar.activation(out=res[:, nb, :], in_=sum_bank[jb][:, nb * P : (nb + 1) * P], func=ACT.Silu,
-                                         bias=cols[:, 4 * G + nb : 4 * G + nb + 1])
-                nc.sync.dma_start(out=out.rearrange("(c p) j -> p c j", p=P)[:, :, jb * P : (jb + 1) * P], in_=res[:])
+                nc.tensor.matmul(sum_bank[jb][:, ns], lhsT=part[key, jb][:, ns], rhs=ident[:], is_transpose=True,
+                                 start=(start and nb == 0), stop=(stop and nb == NB - 1))
 
+        def finish(jb):
+            for c in range(0, NB, 2):
+                res = keep.tile([P, 2, P], F32, name="res%d_%d" % (jb, c))
+                for nb in range(c, c + 2):
+                    nc.scalar.activation(out=res[:, nb - c, :], in_=sum_bank[jb][:, nb * P : (nb + 1) * P],
+                                         func=ACT.Silu, bias=weight(G, nb))
+                nc.sync.dma_start(out=out.rearrange("(c p) j -> p c j", p=P)[:, c : c + 2, jb * P : (jb + 1) * P],
+                                  in_=res[:])
+
+        def after(g, jb):
+            if g == 0 and jb < EARLY:
+                turn(g, jb, False, False)
+            if g == 1 and jb >= EARLY:
+                both = new_part("both", jb)
+                nc.gpsimd.tensor_tensor(out=both[:], in0=part[SKIP, jb][:], in1=part[1, jb][:], op=ALU.add)
+                turn("both", jb, True, False)
+            if g == G - 1:
+                turn(g, jb, False, True)
+                finish(jb)
+
+        interleave_half(0, nc.vector.tensor_copy)
+        quantise_half(0, "x_w0")
+        for g in range(G):
+            nc.vector.tensor_copy(got_s[g][:], tab_s[:].indirect(offsets[:, 32 * g : 32 * (g + 1)]))
+        interleave_half(1, nc.scalar.copy)
+        for jb in range(EARLY):
+            product(SKIP, jb, mx_bank[jb])
+        for jb in range(EARLY):
+            weigh(SKIP, jb, mx_bank[jb])
+            turn(SKIP, jb, True, False)
+        quantise_half(1, "part%s_%d" % (SKIP, EARLY - 1))
+        for g in range(G):
+            nc.vector.tensor_copy(got_w[g][:], tab_w[:].indirect(offsets[:, 32 * g : 32 * (g + 1)]))
+
+        steps = [(SKIP, jb) for jb in range(EARLY, JB)] + [(0, jb) for jb in range(JB)]
+        steps = steps + [(1, 0), (1, 1), (2, 0), (1, 2), (2, 1), (1, 3), (3, 0), (2, 2), (3, 1), (2, 3), (3, 2), (3, 3)]
         for n in range(MX_BANKS):
-            product(n)
-        for n in range(len(steps)):
-            weigh(n)
-            if n == JB - 1:
-                nc.tensor.transpose(mx_bank[n][:, 0:P], rows[:], ident[:])
-                nc.scalar.copy(out=cols[:], in_=mx_bank[n][:, 0 : (G + 1) * 4])
+            product(*steps[n], mx_bank[n])
+        for n, (g, jb) in enumerate(steps):
+            bank = mx_bank[n % MX_BANKS]
+            weigh(g, jb, bank)
+            if n == 0:
+                nc.tensor.transpose(bank[:, 0:P], rows[:], ident[:])
+                nc.scalar.copy(out=cols[:], in_=bank[:, 0 : (G + 1) * 4])
             if n + MX_BANKS < len(steps):
-                product(n + MX_BANKS)
-            turn(n)
+                product(*steps[n + MX_BANKS], bank)
+            after(g, jb)

@@ -52,8 +52,8 @@ def tile_list_interp_silu_kernel(
         got_s = [keep.tile([P, J], U8, name="got_s%d" % g, align_bytes=64) for g in range(G)]
         x_s = [keep.tile([P, HALF], U8, name="x_s%d" % h, align_bytes=64) for h in range(2)]
         got_w = [keep.tile([P, J], U32, name="got_w%d" % g, align_bytes=64) for g in range(G)]
-        rows = keep.tile([P, P], F32, name="rows")
-        cols = keep.tile([P, (G + 1) * 4], F32, name="cols")
+        rows = [keep.tile([P, P], F32, name="rows%d" % i) for i in range(2)]
+        cols = [keep.tile([P, 12], F32, name="cols%d" % i) for i in range(2)]
         ident = keep.tile([P, P], F32, name="ident")
         warm = keep.tile([P, 16], F32, name="warm")
         mx_bank = [psum.tile([P, N], F32, name="mx_bank%d" % i) for i in range(MX_BANKS)]
@@ -64,9 +64,14 @@ def tile_list_interp_silu_kernel(
         nc.gpsimd.memset(tab_s_words[:, 768:1024], 0)
         nc.gpsimd.memset(warm[:, 0:1], 0.0)
         nc.gpsimd.memset(wx_s[:].bitcast(I32), 0)
-        nc.gpsimd.memset(rows[:], 0.0)
+        nc.gpsimd.memset(rows[0][:], 0.0)
         nc.gpsimd.memset(w_s[:].bitcast(I32), 0)
+        nc.gpsimd.memset(rows[1][:], 0.0)
         make_identity(nc, ident[:])
+
+        def load_vectors(dst, vecs):
+            for i, vec in enumerate(vecs):
+                nc.sync.dma_start(out=dst[4 * i : 4 * i + 4, :], in_=vec.rearrange("(c p) -> c p", p=P))
 
         x_rows = x.rearrange("(p t) j -> p t j", t=4)
         nc.sync.dma_start(offsets[:], offs)
@@ -76,11 +81,10 @@ def tile_list_interp_silu_kernel(
         nc.sync.dma_start(out=x_raw[1][:], in_=x_rows[:, :, HALF:J])
         load_scale_rows((nc.sync,) * 4, wx_s, wx_scales[0])
         nc.sync.dma_start(out=tab_w[:].bitcast(I32), in_=tab_words[0].rearrange("p t i -> p (t i)").bitcast(I32))
-        for i, vec in enumerate((iw0, iw1, iw2, iw3, b)):
-            queue = nc.sync if i in (2, 3) else nc.gpsimd
-            queue.dma_start(out=rows[4 * i : 4 * i + 4, :], in_=vec.rearrange("(c p) -> c p", p=P))
+        load_vectors(rows[0], (iw0, iw1))
         nc.sync.dma_start(out=w_w[:].bitcast(I32), in_=w_words[0].bitcast(I32))
         load_scale_rows((nc.sync,) * 4, w_s, w_scales[0])
+        load_vectors(rows[1], (iw2, iw3, b))
 
         nc.scalar.activation(out=warm[:, 8:9], in_=warm[:, 0:1], func=ACT.Silu)
 
@@ -101,7 +105,8 @@ def tile_list_interp_silu_kernel(
             )
 
         def weight(g, jb):
-            return cols[:, 4 * g + jb : 4 * g + jb + 1]
+            i, r = (0, g) if g < 2 else (1, g - 2)
+            return cols[i][:, 4 * r + jb : 4 * r + jb + 1]
 
         def product(g, jb, bank):
             if g == SKIP:
@@ -125,7 +130,7 @@ def tile_list_interp_silu_kernel(
             elif g < 2:
                 nc.scalar.activation(out=dst[:], in_=bank[:], func=ACT.Copy, scale=weight(g, jb))
             else:
-                onto = 0 if g == 2 and jb >= EARLY else g - 1
+                onto = g - 1 if jb < EARLY else (0 if g == 2 else "both")
                 nc.vector.scalar_tensor_tensor(out=dst[:], in0=bank[:], scalar=weight(g, jb),
                                                in1=part[onto, jb][:], op0=ALU.mult, op1=ALU.add)
 
@@ -150,7 +155,8 @@ def tile_list_interp_silu_kernel(
             if g == 1 and jb >= EARLY:
                 both = new_part("both", jb)
                 nc.gpsimd.tensor_tensor(out=both[:], in0=part[SKIP, jb][:], in1=part[1, jb][:], op=ALU.add)
-                turn("both", jb, True, False)
+            if g == 2 and jb >= EARLY:
+                turn(g, jb, True, False)
             if g == G - 1:
                 turn(g, jb, False, True)
                 finish(jb)
@@ -170,15 +176,15 @@ def tile_list_interp_silu_kernel(
             nc.vector.tensor_copy(got_w[g][:], tab_w[:].indirect(offsets[:, 32 * g : 32 * (g + 1)]))
 
         steps = [(SKIP, jb) for jb in range(EARLY, JB)] + [(0, jb) for jb in range(JB)]
-        steps = steps + [(1, 0), (1, 1), (2, 0), (1, 2), (2, 1), (1, 3), (3, 0), (2, 2), (3, 1), (2, 3), (3, 2), (3, 3)]
+        steps = steps + [(1, 0), (1, 2), (2, 0), (1, 1), (2, 2), (1, 3), (3, 0), (2, 1), (3, 2), (2, 3), (3, 1), (3, 3)]
         for n in range(MX_BANKS):
             product(*steps[n], mx_bank[n])
         for n, (g, jb) in enumerate(steps):
             bank = mx_bank[n % MX_BANKS]
             weigh(g, jb, bank)
-            if n == 0:
-                nc.tensor.transpose(bank[:, 0:P], rows[:], ident[:])
-                nc.scalar.copy(out=cols[:], in_=bank[:, 0 : (G + 1) * 4])
+            if n in (0, 3):
+                nc.tensor.transpose(bank[:, 0:P], rows[n // 3][:], ident[:])
+                nc.scalar.copy(out=cols[n // 3][:], in_=bank[:, 0:12])
             if n + MX_BANKS < len(steps):
                 product(*steps[n + MX_BANKS], bank)
             after(g, jb)

@@ -19,17 +19,23 @@ FP4X4 = mybir.dt.float4_e2m1fn_x4
 ACT = mybir.ActivationFunctionType
 ALU = mybir.AluOpType
 
+PACK = 4
 JB = J // P
 NB = N // P
+LIST_COLS = J // 16
 HALF = J // 2
+EARLY = HALF // P
 MX_BANKS = 4
 SKIP = G
-EARLY = HALF // P
+BOTH = "both"
+VECTOR_ZEROES = 768
+VEC_COLS = 3 * JB
+STORE_NB = 2
 
 
-def load_scale_rows(queues, plane, rows):
-    for r, queue in enumerate(queues):
-        queue.dma_start(out=plane[r:P:32, :].bitcast(I32), in_=rows[r:16:4, :].bitcast(I32))
+def load_scale_rows(nc, scale_tile, rows):
+    for r in range(4):
+        nc.sync.dma_start(out=scale_tile[r:P:32, :].bitcast(I32), in_=rows[r:16:4, :].bitcast(I32))
 
 
 def tile_list_interp_silu_kernel(
@@ -40,29 +46,27 @@ def tile_list_interp_silu_kernel(
         keep = ctx.enter_context(tc.tile_pool(name="keep", bufs=1))
         psum = ctx.enter_context(tc.psum_pool(name="psum", bufs=1))
 
-        offsets = keep.tile([P, G * J // 16], U16, name="offsets")
+        offsets = keep.tile([P, G * LIST_COLS], U16, name="offsets")
         tab_w = keep.tile([P, T], U32, name="tab_w", align_bytes=64)
         tab_s = keep.tile([P, T], U8, name="tab_s", align_bytes=64)
         w_w = keep.tile([P, 2 * N], U8, name="w_w", align_bytes=64)
         w_s = keep.tile([P, N], U8, name="w_s", align_bytes=64)
         wx_w = keep.tile([P, N], U32, name="wx_w", align_bytes=64)
         wx_s = keep.tile([P, N], U8, name="wx_s", align_bytes=64)
-        x_raw = [keep.tile([P, 4, HALF], F32, name="x_raw%d" % h) for h in range(2)]
-        x_bf = [keep.tile([P, HALF, 4], BF16, name="x_bf%d" % h, align_bytes=64) for h in range(2)]
+        x_raw = [keep.tile([P, PACK, HALF], F32, name="x_raw%d" % h) for h in range(2)]
+        x_bf = [keep.tile([P, HALF, PACK], BF16, name="x_bf%d" % h, align_bytes=64) for h in range(2)]
         got_s = [keep.tile([P, J], U8, name="got_s%d" % g, align_bytes=64) for g in range(G)]
         x_s = [keep.tile([P, HALF], U8, name="x_s%d" % h, align_bytes=64) for h in range(2)]
         got_w = [keep.tile([P, J], U32, name="got_w%d" % g, align_bytes=64) for g in range(G)]
         rows = [keep.tile([P, P], F32, name="rows%d" % i) for i in range(2)]
-        cols = [keep.tile([P, 12], F32, name="cols%d" % i) for i in range(2)]
+        cols = [keep.tile([P, VEC_COLS], F32, name="cols%d" % i) for i in range(2)]
         ident = keep.tile([P, P], F32, name="ident")
-        warm = keep.tile([P, 16], F32, name="warm")
         mx_bank = [psum.tile([P, N], F32, name="mx_bank%d" % i) for i in range(MX_BANKS)]
         sum_bank = [psum.tile([P, N], F32, name="sum_bank%d" % i) for i in range(JB)]
 
         tab_s_words = tab_s[:].bitcast(I32)
-        nc.vector.memset(tab_s_words[:, 0:768], 0)
-        nc.gpsimd.memset(tab_s_words[:, 768:1024], 0)
-        nc.gpsimd.memset(warm[:, 0:1], 0.0)
+        nc.vector.memset(tab_s_words[:, 0:VECTOR_ZEROES], 0)
+        nc.gpsimd.memset(tab_s_words[:, VECTOR_ZEROES : T // 4], 0)
         nc.gpsimd.memset(wx_s[:].bitcast(I32), 0)
         nc.gpsimd.memset(rows[0][:], 0.0)
         nc.gpsimd.memset(w_s[:].bitcast(I32), 0)
@@ -71,25 +75,26 @@ def tile_list_interp_silu_kernel(
 
         def load_vectors(dst, vecs):
             for i, vec in enumerate(vecs):
-                nc.sync.dma_start(out=dst[4 * i : 4 * i + 4, :], in_=vec.rearrange("(c p) -> c p", p=P))
+                nc.sync.dma_start(out=dst[JB * i : JB * (i + 1), :], in_=vec.rearrange("(c p) -> c p", p=P))
 
-        x_rows = x.rearrange("(p t) j -> p t j", t=4)
+        x_rows = x.rearrange("(p t) j -> p t j", t=PACK)
         nc.sync.dma_start(offsets[:], offs)
         nc.sync.dma_start(out=x_raw[0][:], in_=x_rows[:, :, 0:HALF])
-        load_scale_rows((nc.sync,) * 4, tab_s, tab_scales[0])
+        load_scale_rows(nc, tab_s, tab_scales[0])
         nc.sync.dma_start(out=wx_w[:].bitcast(I32), in_=wx_words[0].rearrange("p n i -> p (n i)").bitcast(I32))
         nc.sync.dma_start(out=x_raw[1][:], in_=x_rows[:, :, HALF:J])
-        load_scale_rows((nc.sync,) * 4, wx_s, wx_scales[0])
+        load_scale_rows(nc, wx_s, wx_scales[0])
         nc.sync.dma_start(out=tab_w[:].bitcast(I32), in_=tab_words[0].rearrange("p t i -> p (t i)").bitcast(I32))
         load_vectors(rows[0], (iw0, iw1))
         nc.sync.dma_start(out=w_w[:].bitcast(I32), in_=w_words[0].bitcast(I32))
-        load_scale_rows((nc.sync,) * 4, w_s, w_scales[0])
+        load_scale_rows(nc, w_s, w_scales[0])
         load_vectors(rows[1], (iw2, iw3, b))
-
-        nc.scalar.activation(out=warm[:, 8:9], in_=warm[:, 0:1], func=ACT.Silu)
 
         x_w = []
         part = {}
+
+        def part_tag(key, jb):
+            return "part%s_%d" % (key, jb)
 
         def interleave_half(h, copy):
             copy(
@@ -104,9 +109,14 @@ def tile_list_interp_silu_kernel(
                 out=words[:].bitcast(FP8X4), scales=x_s[h][:], in_=x_bf[h][:].rearrange("p c t -> p (c t)")
             )
 
-        def weight(g, jb):
-            i, r = (0, g) if g < 2 else (1, g - 2)
-            return cols[i][:, 4 * r + jb : 4 * r + jb + 1]
+        def look_up(got, table):
+            for g in range(G):
+                entries = offsets[:, LIST_COLS * g : LIST_COLS * (g + 1)]
+                nc.vector.tensor_copy(got[g][:], table[:].indirect(entries))
+
+        def vector_column(v, c):
+            i, r = (0, v) if v < 2 else (1, v - 2)
+            return cols[i][:, JB * r + c : JB * r + c + 1]
 
         def product(g, jb, bank):
             if g == SKIP:
@@ -119,7 +129,7 @@ def tile_list_interp_silu_kernel(
                                     rhs=w_w[:].bitcast(FP4X4), rhs_scale=w_s[:], start=True, stop=True)
 
         def new_part(key, jb):
-            dst = keep.tile([P, N], F32, name="part%s_%d" % (key, jb), tag="part%s_%d" % (key, jb), align_bytes=64)
+            dst = keep.tile([P, N], F32, name=part_tag(key, jb), tag=part_tag(key, jb), align_bytes=64)
             part[key, jb] = dst
             return dst
 
@@ -128,10 +138,10 @@ def tile_list_interp_silu_kernel(
             if g == SKIP:
                 nc.scalar.copy(out=dst[:], in_=bank[:])
             elif g < 2:
-                nc.scalar.activation(out=dst[:], in_=bank[:], func=ACT.Copy, scale=weight(g, jb))
+                nc.scalar.activation(out=dst[:], in_=bank[:], func=ACT.Copy, scale=vector_column(g, jb))
             else:
-                onto = g - 1 if jb < EARLY else (0 if g == 2 else "both")
-                nc.vector.scalar_tensor_tensor(out=dst[:], in0=bank[:], scalar=weight(g, jb),
+                onto = g - 1 if jb < EARLY else (0 if g == 2 else BOTH)
+                nc.vector.scalar_tensor_tensor(out=dst[:], in0=bank[:], scalar=vector_column(g, jb),
                                                in1=part[onto, jb][:], op0=ALU.mult, op1=ALU.add)
 
         def turn(key, jb, start, stop):
@@ -140,20 +150,25 @@ def tile_list_interp_silu_kernel(
                 nc.tensor.matmul(sum_bank[jb][:, ns], lhsT=part[key, jb][:, ns], rhs=ident[:], is_transpose=True,
                                  start=(start and nb == 0), stop=(stop and nb == NB - 1))
 
+        def turn_vectors(i, bank):
+            nc.tensor.transpose(bank[:, 0:P], rows[i][:], ident[:])
+            nc.scalar.copy(out=cols[i][:], in_=bank[:, 0:VEC_COLS])
+
         def finish(jb):
-            for c in range(0, NB, 2):
-                res = keep.tile([P, 2, P], F32, name="res%d_%d" % (jb, c))
-                for nb in range(c, c + 2):
+            for c in range(0, NB, STORE_NB):
+                res = keep.tile([P, STORE_NB, P], F32, name="res%d_%d" % (jb, c))
+                for nb in range(c, c + STORE_NB):
                     nc.scalar.activation(out=res[:, nb - c, :], in_=sum_bank[jb][:, nb * P : (nb + 1) * P],
-                                         func=ACT.Silu, bias=weight(G, nb))
-                nc.sync.dma_start(out=out.rearrange("(c p) j -> p c j", p=P)[:, c : c + 2, jb * P : (jb + 1) * P],
-                                  in_=res[:])
+                                         func=ACT.Silu, bias=vector_column(G, nb))
+                nc.sync.dma_start(
+                    out=out.rearrange("(c p) j -> p c j", p=P)[:, c : c + STORE_NB, jb * P : (jb + 1) * P], in_=res[:]
+                )
 
         def after(g, jb):
             if g == 0 and jb < EARLY:
                 turn(g, jb, False, False)
             if g == 1 and jb >= EARLY:
-                both = new_part("both", jb)
+                both = new_part(BOTH, jb)
                 nc.gpsimd.tensor_tensor(out=both[:], in0=part[SKIP, jb][:], in1=part[1, jb][:], op=ALU.add)
             if g == 2 and jb >= EARLY:
                 turn(g, jb, True, False)
@@ -163,28 +178,30 @@ def tile_list_interp_silu_kernel(
 
         interleave_half(0, nc.vector.tensor_copy)
         quantise_half(0, "x_w0")
-        for g in range(G):
-            nc.vector.tensor_copy(got_s[g][:], tab_s[:].indirect(offsets[:, 32 * g : 32 * (g + 1)]))
+        look_up(got_s, tab_s)
         interleave_half(1, nc.scalar.copy)
         for jb in range(EARLY):
             product(SKIP, jb, mx_bank[jb])
         for jb in range(EARLY):
             weigh(SKIP, jb, mx_bank[jb])
             turn(SKIP, jb, True, False)
-        quantise_half(1, "part%s_%d" % (SKIP, EARLY - 1))
-        for g in range(G):
-            nc.vector.tensor_copy(got_w[g][:], tab_w[:].indirect(offsets[:, 32 * g : 32 * (g + 1)]))
+        quantise_half(1, part_tag(SKIP, EARLY - 1))
+        look_up(got_w, tab_w)
 
         steps = [(SKIP, jb) for jb in range(EARLY, JB)] + [(0, jb) for jb in range(JB)]
-        steps = steps + [(1, 0), (1, 2), (2, 0), (1, 1), (2, 2), (1, 3), (3, 0), (2, 1), (3, 2), (2, 3), (3, 1), (3, 3)]
+        blocks = [jb for e in range(EARLY) for jb in (e, EARLY + e)]
+        lags = ((1, 0), (3, 3), (2, 1))
+        for r in range(JB + max(lag for g, lag in lags)):
+            steps = steps + [(g, blocks[r - lag]) for g, lag in lags if 0 <= r - lag < JB]
+        vectors_after = {(SKIP, EARLY): 0, (0, 1): 1}
+
         for n in range(MX_BANKS):
             product(*steps[n], mx_bank[n])
         for n, (g, jb) in enumerate(steps):
             bank = mx_bank[n % MX_BANKS]
             weigh(g, jb, bank)
-            if n in (0, 3):
-                nc.tensor.transpose(bank[:, 0:P], rows[n // 3][:], ident[:])
-                nc.scalar.copy(out=cols[n // 3][:], in_=bank[:, 0:12])
+            if (g, jb) in vectors_after:
+                turn_vectors(vectors_after[g, jb], bank)
             if n + MX_BANKS < len(steps):
                 product(*steps[n + MX_BANKS], bank)
             after(g, jb)

from contextlib import ExitStack

import concourse.mybir as mybir
from concourse.masks import make_identity

K, L, N, T, J = 512, 512, 512, 4096, 512
G = 4
P = 128
FLOPS = 2 * K * N * J * G + 2 * L * N * J

F32 = mybir.dt.float32
BF16 = mybir.dt.bfloat16
I32 = mybir.dt.int32
U32 = mybir.dt.uint32
U16 = mybir.dt.uint16
U8 = mybir.dt.uint8
FP8X4 = mybir.dt.float8_e4m3fn_x4
FP4X4 = mybir.dt.float4_e2m1fn_x4
ACT = mybir.ActivationFunctionType
ALU = mybir.AluOpType

PACK = 4
JB = J // P
NB = N // P
LIST_COLS = J // 16
HALF = J // 2
EARLY = HALF // P
MX_BANKS = 4
SKIP = G
BOTH = "both"
VECTOR_ZEROES = 768
VEC_COLS = 3 * JB
STORE_NB = 2


def load_scale_rows(nc, scale_tile, rows):
    for r in range(4):
        nc.sync.dma_start(out=scale_tile[r:P:32, :].bitcast(I32), in_=rows[r:16:4, :].bitcast(I32))


def tile_list_interp_silu_kernel(
    tc, tab_words, tab_scales, w_words, w_scales, x, wx_words, wx_scales, iw0, iw1, iw2, iw3, b, offs, out
):
    nc = tc.nc
    with ExitStack() as ctx:
        keep = ctx.enter_context(tc.tile_pool(name="keep", bufs=1))
        psum = ctx.enter_context(tc.psum_pool(name="psum", bufs=1))

        offsets = keep.tile([P, G * LIST_COLS], U16, name="offsets")
        tab_w = keep.tile([P, T], U32, name="tab_w", align_bytes=64)
        tab_s = keep.tile([P, T], U8, name="tab_s", align_bytes=64)
        w_w = keep.tile([P, 2 * N], U8, name="w_w", align_bytes=64)
        w_s = keep.tile([P, N], U8, name="w_s", align_bytes=64)
        wx_w = keep.tile([P, N], U32, name="wx_w", align_bytes=64)
        wx_s = keep.tile([P, N], U8, name="wx_s", align_bytes=64)
        x_raw = [keep.tile([P, PACK, HALF], F32, name="x_raw%d" % h) for h in range(2)]
        x_bf = [keep.tile([P, HALF, PACK], BF16, name="x_bf%d" % h, align_bytes=64) for h in range(2)]
        got_s = [keep.tile([P, J], U8, name="got_s%d" % g, align_bytes=64) for g in range(G)]
        x_s = [keep.tile([P, HALF], U8, name="x_s%d" % h, align_bytes=64) for h in range(2)]
        got_w = [keep.tile([P, J], U32, name="got_w%d" % g, align_bytes=64) for g in range(G)]
        rows = [keep.tile([P, P], F32, name="rows%d" % i) for i in range(2)]
        cols = [keep.tile([P, VEC_COLS], F32, name="cols%d" % i) for i in range(2)]
        ident = keep.tile([P, P], F32, name="ident")
        mx_bank = [psum.tile([P, N], F32, name="mx_bank%d" % i) for i in range(MX_BANKS)]
        sum_bank = [psum.tile([P, N], F32, name="sum_bank%d" % i) for i in range(JB)]

        tab_s_words = tab_s[:].bitcast(I32)
        nc.vector.memset(tab_s_words[:, 0:VECTOR_ZEROES], 0)
        nc.gpsimd.memset(tab_s_words[:, VECTOR_ZEROES : T // 4], 0)
        nc.gpsimd.memset(wx_s[:].bitcast(I32), 0)
        nc.gpsimd.memset(rows[0][:], 0.0)
        nc.gpsimd.memset(w_s[:].bitcast(I32), 0)
        nc.gpsimd.memset(rows[1][:], 0.0)
        make_identity(nc, ident[:])

        def load_vectors(dst, vecs):
            for i, vec in enumerate(vecs):
                nc.sync.dma_start(out=dst[JB * i : JB * (i + 1), :], in_=vec.rearrange("(c p) -> c p", p=P))

        x_rows = x.rearrange("(p t) j -> p t j", t=PACK)
        nc.sync.dma_start(offsets[:], offs)
        nc.sync.dma_start(out=x_raw[0][:], in_=x_rows[:, :, 0:HALF])
        load_scale_rows(nc, tab_s, tab_scales[0])
        nc.sync.dma_start(out=wx_w[:].bitcast(I32), in_=wx_words[0].rearrange("p n i -> p (n i)").bitcast(I32))
        nc.sync.dma_start(out=x_raw[1][:], in_=x_rows[:, :, HALF:J])
        load_scale_rows(nc, wx_s, wx_scales[0])
        nc.sync.dma_start(out=tab_w[:].bitcast(I32), in_=tab_words[0].rearrange("p t i -> p (t i)").bitcast(I32))
        load_vectors(rows[0], (iw0, iw1))
        nc.sync.dma_start(out=w_w[:].bitcast(I32), in_=w_words[0].bitcast(I32))
        load_scale_rows(nc, w_s, w_scales[0])
        load_vectors(rows[1], (iw2, iw3, b))

        x_w = []
        part = {}

        def part_tag(key, jb):
            return "part%s_%d" % (key, jb)

        def interleave_half(h, copy):
            copy(
                out=x_bf[h][:].rearrange("p (c i) t -> p c t i", i=4),
                in_=x_raw[h][:].rearrange("p t (c i) -> p c t i", i=4),
            )

        def quantise_half(h, tag):
            words = keep.tile([P, HALF], U32, name="x_w%d" % h, tag=tag, align_bytes=64)
            x_w.append(words)
            nc.vector.quantize_mx(
                out=words[:].bitcast(FP8X4), scales=x_s[h][:], in_=x_bf[h][:].rearrange("p c t -> p (c t)")
            )

        def look_up(got, table):
            for g in range(G):
                entries = offsets[:, LIST_COLS * g : LIST_COLS * (g + 1)]
                nc.vector.tensor_copy(got[g][:], table[:].indirect(entries))

        def vector_column(v, c):
            i, r = (0, v) if v < 2 else (1, v - 2)
            return cols[i][:, JB * r + c : JB * r + c + 1]

        def product(g, jb, bank):
            if g == SKIP:
                h, c = divmod(jb * P, HALF)
                nc.tensor.matmul_mx(bank[:], lhsT=x_w[h][:, c : c + P].bitcast(FP8X4), lhsT_scale=x_s[h][:, c : c + P],
                                    rhs=wx_w[:].bitcast(FP8X4), rhs_scale=wx_s[:], start=True, stop=True)
            else:
                js = slice(jb * P, (jb + 1) * P)
                nc.tensor.matmul_mx(bank[:], lhsT=got_w[g][:, js].bitcast(FP8X4), lhsT_scale=got_s[g][:, js],
                                    rhs=w_w[:].bitcast(FP4X4), rhs_scale=w_s[:], start=True, stop=True)

        def new_part(key, jb):
            dst = keep.tile([P, N], F32, name=part_tag(key, jb), tag=part_tag(key, jb), align_bytes=64)
            part[key, jb] = dst
            return dst

        def weigh(g, jb, bank):
            dst = new_part(g, jb)
            if g == SKIP:
                nc.scalar.copy(out=dst[:], in_=bank[:])
            elif g < 2:
                nc.scalar.activation(out=dst[:], in_=bank[:], func=ACT.Copy, scale=vector_column(g, jb))
            else:
                onto = g - 1 if jb < EARLY else (0 if g == 2 else BOTH)
                nc.vector.scalar_tensor_tensor(out=dst[:], in0=bank[:], scalar=vector_column(g, jb),
                                               in1=part[onto, jb][:], op0=ALU.mult, op1=ALU.add)

        def turn(key, jb, start, stop):
            for nb in range(NB):
                ns = slice(nb * P, (nb + 1) * P)
                nc.tensor.matmul(sum_bank[jb][:, ns], lhsT=part[key, jb][:, ns], rhs=ident[:], is_transpose=True,
                                 start=(start and nb == 0), stop=(stop and nb == NB - 1))

        def turn_vectors(i, bank):
            nc.tensor.transpose(bank[:, 0:P], rows[i][:], ident[:])
            nc.scalar.copy(out=cols[i][:], in_=bank[:, 0:VEC_COLS])

        def finish(jb):
            for c in range(0, NB, STORE_NB):
                res = keep.tile([P, STORE_NB, P], F32, name="res%d_%d" % (jb, c))
                for nb in range(c, c + STORE_NB):
                    nc.scalar.activation(out=res[:, nb - c, :], in_=sum_bank[jb][:, nb * P : (nb + 1) * P],
                                         func=ACT.Silu, bias=vector_column(G, nb))
                nc.sync.dma_start(
                    out=out.rearrange("(c p) j -> p c j", p=P)[:, c : c + STORE_NB, jb * P : (jb + 1) * P], in_=res[:]
                )

        def after(g, jb):
            if g == 0 and jb < EARLY:
                turn(g, jb, False, False)
            if g == 1 and jb >= EARLY:
                both = new_part(BOTH, jb)
                nc.gpsimd.tensor_tensor(out=both[:], in0=part[SKIP, jb][:], in1=part[1, jb][:], op=ALU.add)
            if g == 2 and jb >= EARLY:
                turn(g, jb, True, False)
            if g == G - 1:
                turn(g, jb, False, True)
                finish(jb)

        interleave_half(0, nc.vector.tensor_copy)
        quantise_half(0, "x_w0")
        look_up(got_s, tab_s)
        interleave_half(1, nc.scalar.copy)
        for jb in range(EARLY):
            product(SKIP, jb, mx_bank[jb])
        for jb in range(EARLY):
            weigh(SKIP, jb, mx_bank[jb])
            turn(SKIP, jb, True, False)
        quantise_half(1, part_tag(SKIP, EARLY - 1))
        look_up(got_w, tab_w)

        steps = [(SKIP, jb) for jb in range(EARLY, JB)] + [(0, jb) for jb in range(JB)]
        blocks = [jb for e in range(EARLY) for jb in (e, EARLY + e)]
        lags = ((1, 0), (3, 3), (2, 1))
        for r in range(JB + max(lag for g, lag in lags)):
            steps = steps + [(g, blocks[r - lag]) for g, lag in lags if 0 <= r - lag < JB]
        vectors_after = {(SKIP, EARLY): 0, (0, 1): 1}

        for n in range(MX_BANKS):
            product(*steps[n], mx_bank[n])
        for n, (g, jb) in enumerate(steps):
            bank = mx_bank[n % MX_BANKS]
            weigh(g, jb, bank)
            if (g, jb) in vectors_after:
                turn_vectors(vectors_after[g, jb], bank)
            if n + MX_BANKS < len(steps):
                product(*steps[n + MX_BANKS], bank)
            after(g, jb)
